import numpy as np, ml_dtypes
CORES = [23,119,17,113]
N = 4
BF = ml_dtypes.bfloat16
V, C, S, IT, Q, RO, D = 2048, 256, 256, 4, 9, 2, 2048
P = V + 2 * C * RO
def mesh(rng, m, isb, chain):
    o = rng.permutation(V); x = np.zeros(3 * V, np.int64); sn = np.zeros(2 * S, np.int64); rest = V - 2 * m
    x[2 * V + o[0:2 * m:2]] = o[1:2 * m:2]; x[2 * V + o[1:2 * m:2]] = o[0:2 * m:2]
    up = 2 * V + o[2 * m:]; leg = rng.integers(0, 2, rest) * V + o[:rest] if chain else rng.permutation(2 * V)[:rest]
    left = np.ones(2 * V, bool); left[leg] = False
    jb, jl = np.flatnonzero(isb), np.flatnonzero(~isb); c = rng.permutation(rest); cut, keep = c[:len(jb)], c[len(jb):]
    x[up[keep]] = leg[keep] % V; x[leg[keep]] = up[keep] - 2 * V
    x[up[cut]] = P + jb; sn[jb] = up[cut] - 2 * V
    pool = np.concatenate([rng.permutation(leg[cut]), rng.permutation(np.flatnonzero(left))]); h = rng.permutation(pool[:len(jl)])
    x[h] = P + jl; sn[jl] = h % V
    k = rng.permutation(pool[len(jl):]).reshape(2, -1); x[k[0]] = k[1] % V; x[k[1]] = k[0] % V
    return x.reshape(3, V), sn, o
def meshes(rng, m, chain=False):
    x = rng.choice(4, (N, 8, S), p=[0.35, 0.35, 0.2, 0.1])
    isb = np.concatenate([np.roll((x == 1) | (x == 3), 1, axis=0), (x == 0) | (x == 3)], axis=2)
    z = [[mesh(rng, int(m[a, g]), isb[a, g], chain) for g in range(8)] for a in range(N)]
    return tuple(np.stack([np.stack([u[i] for u in row]) for row in z]) for i in range(3))
def levels(rng):
    return rng.permuted(np.tile(np.array([60, 90, 110, 130, 150, 165, 180, 200]), (N, 1)), axis=1)[:, :, None, None] + rng.integers(-20, 21, (N, 8, 16, 1))
def errors(rng):
    return (256 * (0.25 + 0.75 * rng.random((N, 8, 1, V))) * rng.random((N, 8, 16, V))).astype(np.int64)
def under(rng, th):
    return np.minimum((th * rng.random((N, 8, 16, V))).astype(np.int64), th - 1)
def plant(rng, e, t, x, y, cnt):
    on = np.argsort(rng.random((16, len(x))), axis=0) < cnt[None, :]; one = rng.random(on.shape) < 0.5
    v = np.where(rng.random(on.shape) < 0.5, t, np.minimum(t + (rng.random(on.shape) * (256 - t)).astype(np.int64), 255))
    e[:, x] = np.where(on & one, v, e[:, x]); e[:, y] = np.where(on & ~one, v, e[:, y])
def more(rng):
    return rng.integers(0, 256, (N, 8, 16, D)), rng.integers(0, 256, (N, 8, 16, 1))
def pack(err, p, sn, det, wt, th):
    b = lambda a: np.ascontiguousarray(a.reshape(N, 128, -1)).astype(np.float32).astype(BF)
    i = lambda a: np.ascontiguousarray(a).astype(np.int32)
    return {"err": b(err), "lt": i(p[:, :, 0]), "rt": i(p[:, :, 1]), "bs": i(p[:, :, 2]), "snd": i(sn), "det": b(det), "wt": i(wt.reshape(N, 128, 1)), "th": i(th.reshape(N, 128, 1))}
def setup_inputs(rng):
    p, sn, o = meshes(rng, rng.integers(V // 8, V // 3 + 1, (N, 8))); det, wt = more(rng)
    return pack(errors(rng), p, sn, det, wt, levels(rng))
def setup_inputs_room(rng):
    M = V // 3; p, sn, o = meshes(rng, np.full((N, 8), M)); det, wt = more(rng)
    th = np.repeat(rng.integers(64, 192, (1, 8, 16, 1)), N, axis=0); err = under(rng, th)
    for a in range(N):
        for g in range(8):
            n = (C, C + 1, 0, 1, C - 1, M, C, C + 1)[(a + g) % 8]
            plant(rng, err[a, g], th[a, g], o[a, g, 0:2 * M:2], o[a, g, 1:2 * M:2], np.where(rng.permutation(M) < n, Q, Q - 1))
    return pack(err, p, sn, det, wt, th)
def setup_inputs_chain(rng):
    M = V // (2 * (IT + 3)); p, sn, o = meshes(rng, np.full((N, 8), M), True); det, wt = more(rng)
    th = np.repeat(rng.integers(64, 192, (1, 8, 16, 1)), N, axis=0); err = under(rng, th); far = np.array([0, 1, IT - 1, IT, IT, IT + 1, IT + 1])
    for a in range(N):
        for g in range(8):
            i = 2 * np.arange(M) + 2 * M * rng.permuted(np.resize(far, M))
            plant(rng, err[a, g], th[a, g], o[a, g, i], o[a, g, i + 1], np.where(rng.random(M) < 0.8, Q, Q - 1))
    return pack(err, p, sn, det, wt, th)
def setup_inputs_ties(rng):
    p, sn, o = meshes(rng, rng.integers(V // 8, V // 3 + 1, (N, 8))); det, wt = more(rng)
    th = np.clip(np.array([1, 2, 100, 128, 254, 255, 255, 30])[None, :, None, None] + rng.integers(-1, 2, (N, 8, 16, 1)), 1, 255); th[:, 6] = 255
    err = np.clip(th - 1 + (rng.random((N, 8, 16, V)) < 0.5 * rng.random((N, 8, 1, V))) * rng.integers(1, 3, (N, 8, 16, V)), 0, 255)
    err[:, 6] = np.minimum(err[:, 6], 254); err[:, 7] = 255
    det[:, 1] = 255; det[:, 2] = 0; wt[:, 0] = 0; wt[:, 1] = 255
    return pack(err, p, sn, det, wt, th)
def pools(rng):
    return [[int(z) for z in rng.permutation(V)] for a in range(N)], rng.permutation(S)[:8 * N].reshape(N, 2, 4)
def watch(x, leg, u, v, slot):
    x[leg, u] = P + slot; x[1 - leg, u] = v; x[2, u] = v; x[:, v] = u
def renamed(rng, x, sn, e):
    pool, kk = pools(rng)
    for a in range(N):
        for s in range(2):
            k, k2, kb, kb2 = [int(z) for z in kk[a, s]]; q, z = (a + 2 * s - 1) % N, (a - 2 * s + 1) % N
            t, b = pool[a].pop(), pool[a].pop()
            x[a, 2, t] = b; x[a, 2, b] = t; x[a, 0, t] = P + (1 - s) * S + k2; x[a, 1, t] = P + s * S + k; e[a, :, t] = 255
            sn[a, s * S + k] = t; sn[a, (1 - s) * S + k] = t
            u, v = pool[q].pop(), pool[q].pop(); sn[q, (1 - s) * S + k] = u; watch(x[q], s, u, v, (1 - s) * S + k)
            u, v = pool[z].pop(), pool[z].pop(); sn[z, s * S + k2] = u; watch(x[z], 1 - s, u, v, s * S + k)
            t, b = pool[a].pop(), pool[a].pop()
            x[a, 2, t] = b; x[a, 2, b] = t; x[a, 0, t] = P + s * S + kb2; e[a, :, t] = 255
            x[a, 1, t] = (P + s * S + kb) % (2 * S) + 2 * S * int(rng.integers(0, V // (2 * S))); sn[a, s * S + kb] = t
            u, v = pool[q].pop(), pool[q].pop(); sn[q, (1 - s) * S + kb2] = u; watch(x[q], s, u, v, (1 - s) * S + kb)
def allpairs(rng, x, e):
    for a in range(N):
        pr = np.sort(rng.permutation(V).reshape(-1, 2), axis=1); pr = pr[np.argsort(pr[:, 0])]
        x[a, 0, pr[0::2]] = pr[1::2]; x[a, 0, pr[1::2]] = pr[0::2]
        for i in (1, 2):
            x[a, i, pr[:, 0]] = pr[:, 1]; x[a, i, pr[:, 1]] = pr[:, 0]
        e[a][:, pr[len(pr) - C // 2:].reshape(-1)] = 255
def crowded(rng, x, sn, e):
    pool, kk = pools(rng)
    for a in range(N):
        for s in range(2):
            q = (a + 2 * s - 1) % N
            for i in range(2):
                k, kn = int(kk[a, s, 2 * i]), int(kk[a, s, 2 * i + 1]); many = [pool[a].pop() for z in range(V // 16)]
                x[a, 2, np.array(many)] = P + s * S + kn
                t = max(many) if i == 0 else min(many); e[a, :, t] = 255; sn[a, s * S + k] = t
                u, v = pool[q].pop(), pool[q].pop(); sn[q, (1 - s) * S + kn] = u; watch(x[q], 1 - i, u, v, (1 - s) * S + k)
def newbases(rng, x, sn, e, th):
    pool, kk = pools(rng)
    for a in range(N):
        pr = np.sort(np.array(pool[a][:2 * S]).reshape(S, 2), axis=1); pr = pr[np.argsort(pr[:, 0])]
        x[a, 2, pr[:, 0]] = pr[:, 1]; x[a, 2, pr[:, 1]] = pr[:, 0]
        plant(rng, e[a], th[a], pr[:, 0], pr[:, 1], rng.integers(Q, 17, S))
        for s in range(2):
            q = (a + 2 * s - 1) % N
            for i in range(2):
                k, kn = int(kk[a, s, 2 * i]), int(kk[a, s, 2 * i + 1]); j = (s * S + kn + P - V) % (2 * S)
                y = int(pr[j // 2, j % 2]); w = pool[a].pop()
                x[a, :, w] = y; x[a, 1, y] = w; e[a, :, w] = 255; sn[a, s * S + k] = w
                u, v = pool[q].pop(), pool[q].pop(); sn[q, (1 - s) * S + kn] = u; watch(x[q], i, u, v, (1 - s) * S + k)
def setup_inputs_free(rng):
    p = rng.choice(np.concatenate([np.arange(V), P + np.arange(2 * S)]), (N, 8, 3, V)); sn = rng.integers(0, V, (N, 8, 2 * S)); m = V // 4
    det, wt = more(rng); err = errors(rng); th = levels(rng)
    for a in range(N):
        for g in range(0, 8, 2):
            o = rng.permutation(V); x = p[a, g]; x[2, o[0:2 * m:2]] = o[1:2 * m:2]; x[2, o[1:2 * m:2]] = o[0:2 * m:2]
            v = o[2 * m:]; v = v[x[2, v] < V]; x[rng.integers(0, 2, len(v)), x[2, v]] = v
            x[0, o[:40]] = o[:40]; x[1, o[20:60]] = o[20:60]; x[0, o[100:140]] = x[1, o[100:140]]; x[1, o[200:240:2]] = o[201:240:2]
            j = rng.permutation(2 * S)[:S // 2]; x[1, sn[a, g, j]] = P + j
    for a in range(N):
        for g in range(0, 8, 2):
            for s in range(2):
                q = (a + 2 * s - 1) % N; k = rng.integers(0, S, 32); k2 = rng.integers(0, S, 32)
                p[q, g, 2, sn[q, g, (1 - s) * S + k]] = P + (1 - s) * S + k2
                p[a, g, rng.integers(0, 2, 32), sn[a, g, s * S + k2]] = P + s * S + k
    p[:, 0, 2, 0] = V - 1; p[:, 0, 2, V - 1] = 0; err[:, 0, :, 0] = 255; err[:, 0, :, V - 1] = 255
    n = 16; me = np.arange(V); two, lone = {}, {}
    for a in range(N):
        for g in range(0, 8, 2):
            x = p[a, g]
            b = np.minimum(x[2], V - 1); pair = (x[2] < V) & (x[2, b] == me) & (b != me)
            t = rng.permutation(np.flatnonzero(pair & (me < b) & (me > 0)))
            two[a, g] = rng.permuted(np.stack([t[:2 * n], b[t[:2 * n]]]), axis=0)
            lone[a, g] = rng.permutation(np.flatnonzero(~pair & (me > 0) & (me < V - 1)))[:2 * n]
            cut = t[C - 4 * n:]; x[2, cut] = P + rng.integers(0, 2 * S, len(cut))
    for g in range(0, 8, 2):
        k, k2 = rng.permutation(S)[:2 * n].reshape(2, n)
        for a in range(N):
            for s in range(2):
                q = (a + 2 * s - 1) % N; u, v = two[a, g][:, s * n:(s + 1) * n]; w = lone[q, g][(1 - s) * n:(2 - s) * n]
                sn[a, g, s * S + k2] = u; sn[q, g, (1 - s) * S + k] = w
                x = p[a, g]; x[0, u] = P + s * S + k; x[1, u] = v; x[0, v] = u; x[1, v] = u
                p[q, g, 2, w] = np.where(np.arange(n) < n // 2, P + s * S + k2, (P + k2) % S + S * rng.integers(0, V // S, n))
                e = err[a, g]; c = np.concatenate([u, v]); e[:, c] = np.minimum(e[:, c], th[a, g] - 1)
                plant(rng, err[q, g], th[a, g], w, w, rng.integers(Q, 17, n))
    th[:, 1::2] = rng.integers(20, 121, (N, 4, 16, 1)); err[:, 1::2] = under(rng, th)[:, 1::2]
    p[:, 1::2, 2] = P + rng.integers(0, 2 * S, (N, 4, V)); p[:, 5] = P + rng.integers(0, 2 * S, (N, 3, V))
    sn[:, 5] = rng.choice(np.array([0, V - 1, V // 2, 5]), (N, 2 * S))
    renamed(rng, p[:, 1], sn[:, 1], err[:, 1]); allpairs(rng, p[:, 3], err[:, 3])
    crowded(rng, p[:, 5], sn[:, 5], err[:, 5]); newbases(rng, p[:, 7], sn[:, 7], err[:, 7], th[:, 7])
    return pack(err, p, sn, det, wt, th)
def setup_inputs_spread(rng):
    p, sn, o = meshes(rng, rng.integers(V // 8, V // 3 + 1, (N, 8)))
    err = (np.exp2(8 * rng.random((N, 8, 1, V))) * rng.random((N, 8, 16, V))).astype(np.int64)
    det = (np.exp2(8 * rng.random((N, 8, 1, D))) * rng.random((N, 8, 16, D))).astype(np.int64)
    wt = np.minimum(np.exp2(8 * rng.random((N, 8, 16, 1))).astype(np.int64), 255)
    th = np.clip(np.exp2(3 + 5 * rng.random((N, 8, 1, 1)) + rng.random((N, 8, 16, 1)) - 0.5).astype(np.int64), 1, 255)
    return pack(np.minimum(err, 255), p, sn, np.minimum(det, 255), wt, th)
def check_inputs(d):
    bad = []
    for k in ("err", "det"):
        x = np.asarray(d[k]).astype(np.float32)
        if not np.all((x >= 0) & (x <= 255) & (x == np.floor(x))): bad.append("range of " + k)
    for k in ("lt", "rt", "bs"):
        x = d[k]
        if not np.all(((x >= 0) & (x < V)) | ((x >= P) & (x < P + 2 * S))): bad.append("range of " + k)
    for k, lo, hi in (("snd", 0, V - 1), ("wt", 0, 255), ("th", 1, 255)):
        if np.min(d[k]) < lo or np.max(d[k]) > hi: bad.append("range of " + k)
    return bad
def ghosts(x):
    return np.concatenate([np.roll(x[..., S:], 1, axis=0), np.roll(x[..., :S], -1, axis=0)], axis=-1)
def reference(err, lt, rt, bs, snd, det, wt, th):
    take = np.take_along_axis; me = np.arange(P)
    e = np.zeros((N, 8, 16, P), np.int32); e[..., :V] = err.astype(np.float32).astype(np.int32).reshape(N, 8, 16, V)
    dt = det.astype(np.float32).astype(np.int32).reshape(N, 8, 16, D); wq = wt.astype(np.int32).reshape(N, 8, 16, 1); tq = th.astype(np.int32).reshape(N, 8, 16, 1)
    p = np.zeros((N, 8, 3, P), np.int64) + me
    p[:, :, 0, :V] = lt; p[:, :, 1, :V] = rt; p[:, :, 2, :V] = bs
    sn = snd.astype(np.int64)
    lo = np.repeat(np.array([0, S]), S); off = np.repeat(np.array([-S, S]), S)
    for t in range(RO):
        L, R, B = p[:, :, 0], p[:, :, 1], p[:, :, 2]
        j = ghosts(take(B, sn, 2)) - P + off
        gb = np.where((j >= lo) & (j < lo + S), take(sn, np.clip(j, 0, 2 * S - 1), 2), -1)
        base = np.concatenate([B, gb], axis=2); gl = (take(base, L, 2) == me)[:, :, None]; gr = (take(base, R, 2) == me)[:, :, None]
        W = e
        for it in range(IT):
            A = np.concatenate([W, ghosts(take(W, sn[:, :, None], 3))], axis=3)
            W = np.maximum(W, np.maximum(np.where(gl, take(A, L[:, :, None], 3), 0), np.where(gr, take(A, R[:, :, None], 3), 0)))
        bo = np.minimum(B, P - 1); pair = (B < P) & (take(B, bo, 2) == me) & (me < B)
        rows = np.add.reduce((np.maximum(W, take(W, bo[:, :, None], 3)) >= tq).astype(np.int32), axis=2)
        go = (pair & (rows >= Q)).astype(np.int64); k = np.add.accumulate(go, axis=2) - go
        a, g, x = np.nonzero((go == 1) & (k < C)); y = B[a, g, x]
        new = np.zeros((N, 8, P), np.int64)
        new[a, g, x] = V + 2 * C * t + 2 * k[a, g, x]; new[a, g, y] = new[a, g, x] + 1
        nx = np.concatenate([new, np.zeros((N, 8, 2 * S), np.int64)], axis=2); rx = np.concatenate([R, np.full((N, 8, 2 * S), -1)], axis=2)
        pn = np.stack([np.where((take(nx, T, 2) > 0) & (take(rx, T, 2) == me), take(nx, T, 2), T) for T in (L, R, B)], axis=2)
        sn = np.where((take(new, sn, 2) > 0) & (take(R, sn, 2) == P + np.arange(2 * S)), take(new, sn, 2), sn)
        a = np.concatenate([a, a]); g = np.concatenate([g, g]); s = np.concatenate([x, y]); o = np.concatenate([y, x])
        n, m = new[a, g, s], new[a, g, o]; bl, br = pn[a, g, 0, s], pn[a, g, 1, s]
        pn[a, g, 0, s] = n; pn[a, g, 1, s] = m; pn[a, g, 2, s] = bl
        pn[a, g, 0, n] = o; pn[a, g, 1, n] = s; pn[a, g, 2, n] = br
        p = pn
        es = e[a, g, :, s]; h = np.add.reduce(wq * e, axis=2)[a, g, s]
        for place in (s, n):
            e[a, g, :, place] = (es >> 1) + (dt[a, g, :, (h + place) & (D - 1)] >> 1)
    return {"ye": e.reshape(N, 128, P).astype(np.float32).astype(BF), "yl": p[:, :, 0].astype(np.float32), "yr": p[:, :, 1].astype(np.float32), "yb": p[:, :, 2].astype(np.float32)}

from concourse.bass import DstId, RemoteDMATransfer
from concourse.mybir import AluOpType as O, ActivationFunctionType as F

V, P, G, Q = 2048, 3072, 3584, 9
WW = G + 16
ZW = 143
bf, f4, i4, u2 = "bfloat16", "float32", "int32", "uint16"
NCH = {0: (1, 2, 2, 1), 1: (1, 2, 2, 1)}


def _s(n, d):
    return ("sbuf", [128, n], d)


SCRATCH = {}
PACK = {}
WIDTH = {}


def _tiles():
    tiles = {
        i4: "IP 1 IG 1 II 1 IJ 1 IM 128 IM2 32 ISi 32 SNI 32 THI 1 WTI 1 MEN 128 MEN2 32 hx 64 hy 64",
        f4: "IXX 143 IL 160 IK 128 ILs 32 IS 32 pc 1 gc 1 jc 4 jj 1 ZF 143 MEL 160 MELm 160 D256 160 MEW 160 OWN 64 OWL 64 mA 128 mB 128 mE 128 mD 128 thc 1 wtc 1 "
            "PE 64 SN1 32 SNLf 32 gt 32 BLm 160 LM 160 RM 160 SLM 32 SRM 32 RSq 32 RSn 32 ea 160 eb 160 pa 160 pb 160 pr 160 pt 160 TH9 160 ones 160 sc 160 kk 160 c8 160 "
            "TF 32 em 32 hz 64 TN 32 ON 32 e1 32 e2 32 e3 32 nz 160 zz 160 nq 160 pz 160 sq 32",
        bf: "ZA 143 ZB 143 ZR 143 ZL 143 ZM 143 ZH 143 BLK 128 NLE 128 IDN 128 N4K 128 MHI 128 MLO 128 OHI 64 OLO 64 PEH 64 PEL 64 SH 32 SL_ 32 SH1 32 SL1 32 go 160",
        u2: "SNL 32 BL 160 LL 160 RL 160 GL 160 GR 160 SL 32 SR 32 PB 160 TG 160 TD 32 HX 64",
    }
    for d, names in tiles.items():
        w = names.split()
        o = 0
        for k, n in zip(w[0::2], w[1::2]):
            PACK[k] = ("pk" + d, o)
            WIDTH[k] = int(n)
            o += (int(n) + 15) // 16 * 16
        SCRATCH["pk" + d] = _s(o, d)
    big = {
        i4: "PI 384",
        f4: "PF0 384 PF1 480 PF2 576 F3 480 q3 480",
        bf: "HI 384 LO 384 HI1 480 LO1 480 TAB0 3584 TAB1 3584 SNDT0 576 SNDT1 576 E 3600 W1 3600 W2 3600 W3 3600 W4 2576 ED 2560 WD 1536 M 2560 FL 2560 AB 2560 AC 2560 X 2560 "
            "OUTL 2560 OUTR 3072 OUTB 2560 NL 2560 NR 3072 NB 2560 OBS 512 OSL 512 OSR 512 ONS 512 NEW0 3584 NEW1 3584 MC0 512 MC1 512 CMP0 2816 CMP1 2816 "
            "DR 2048 DX 2048 DT 2064 ET 512 E2 512 CL 512 OT 512 ORT 512 ONT 512 CZ 1024 " + " ".join("BB%d%d 512" % (t, k) for t in range(2) for k in range(4)),
        u2: "GO0 32 GO1 32 GI0 32 GI1 32",
    }
    for d, names in big.items():
        w = names.split()
        for k, n in zip(w[0::2], w[1::2]):
            WIDTH[k] = int(n)
            SCRATCH[k] = _s(int(n), d)
    for k in range(8):
        WIDTH["ps%d" % k] = 512
        SCRATCH["ps%d" % k] = ("psum", [128, 512], f4)


_tiles()
SEMAPHORES = ["sV", "sS", "sP", "sG", "sX", "gi0", "gi1"] + ["ga%d%d" % (t, k) for t in range(2) for k in range(4)] + ["d%d" % k for k in range(40)]


def rank_program(g, core, T, topo):
    rank = T.rank_of(core)
    if rank is None:
        return
    eng = {"V": g.vector, "S": g.scalar, "P": g.tensor, "G": g, "Y": g.sync}
    count = {"V": 0, "S": 0, "P": 0, "G": 0}
    seen = {q: {} for q in eng}
    hist = {}
    dcount = {}
    closed = set()

    def wait(q, tok):
        sem, val, clock = tok
        if sem in dcount:
            val = dcount[sem]
            closed.add(sem)
        if seen[q].get(sem, 0) < val:
            eng[q].wait_ge(T.sem[sem], val)
            seen[q][sem] = val
        for s, v in clock.items():
            if seen[q].get(s, 0) < v:
                seen[q][s] = v

    def deps(q, reads, writes):
        toks = []
        for kind, regs in (("r", reads), ("w", writes)):
            for b, lo, hi, row in regs:
                ps = b.startswith("ps")
                for rlo, rhi, rrow, rk, rq, tok in hist.get(b, []):
                    if rlo >= hi or lo >= rhi or (row is not None and rrow is not None and row != rrow):
                        continue
                    if rk == "r" and kind == "r" and not (ps and rq != q):
                        continue
                    if rq == q and q == "P" and kind == "w":
                        continue
                    toks.append(tok)
        toks.sort(key=lambda t: -t[1])
        for t in toks:
            wait(q, t)

    def note(q, reads, writes, tok):
        for kind, regs in (("w", writes), ("r", reads)):
            for b, lo, hi, row in regs:
                h = hist.setdefault(b, [])
                if kind == "w" and row is None:
                    h[:] = [r for r in h if not (lo <= r[0] and r[1] <= hi)]
                h.append((lo, hi, row, kind, q, tok))

    def loc(b):
        return PACK.get(b, (b, 0))

    def A(b, lo=None, hi=None, st=1):
        if lo is None:
            lo, hi = 0, WIDTH[b]
        return ("a", b, lo, hi, st)

    def IN(b, lo, hi, ob, c0, c1):
        return ("i", b, lo, hi, ob, c0, c1)

    def mk(x):
        if not isinstance(x, tuple):
            return x
        b, o = loc(x[1])
        if x[0] == "a":
            if x[4] == 1:
                return T[b][:, o + x[2]:o + x[3]]
            return T[b][:, o + x[2]:o + x[3]:x[4]]
        ob, oo = loc(x[4])
        return T[b][:, o + x[2]:o + x[3]].indirect(T[ob][:, oo + x[5]:oo + x[6]])

    def regs(x):
        if not isinstance(x, tuple):
            return []
        b, o = loc(x[1])
        return [(b, 0, 512, None) if b.startswith("ps") else (b, o + x[2], o + x[3], None)]

    def offs(x):
        if isinstance(x, tuple) and x[0] == "i":
            ob, oo = loc(x[4])
            return [(ob, oo + x[5], oo + x[6], None)]
        return []

    def call(q, fn, outs, ins):
        reads = [r for x in ins for r in regs(x) + offs(x)] + [r for x in outs for r in offs(x)]
        writes = [r for x in outs for r in regs(x)]
        deps(q, reads, writes)
        sem = "s" + q
        count[q] += 1
        fn(eng[q]).then_inc(T.sem[sem], 1)
        ck = dict(seen[q])
        ck[sem] = count[q]
        note(q, reads, writes, (sem, count[q], ck))

    def copy(out, in_):
        call("V", lambda e: e.tensor_copy(mk(out), mk(in_)), [out], [in_])

    def scopy(out, in_):
        call("S", lambda e: e.activation(mk(out), mk(in_), F.Copy), [out], [in_])

    def slin(out, in_, scale, bias):
        call("S", lambda e: e.activation(mk(out), mk(in_), F.Identity, bias=bias, scale=scale), [out], [in_])

    def fill(out, c):
        call("V", lambda e: e.memset(mk(out), c), [out], [])

    def tt(out, a, b, op):
        call("V", lambda e: e.tensor_tensor(mk(out), mk(a), mk(b), op), [out], [a, b])

    def ts(out, a, s1, op0, s2=None, op1=None):
        if op1 is None:
            call("V", lambda e: e.tensor_scalar(mk(out), mk(a), mk(s1), None, op0), [out], [a, s1])
        else:
            call("V", lambda e: e.tensor_scalar(mk(out), mk(a), mk(s1), mk(s2), op0, op1), [out], [a, s1, s2])

    def iota(out, pat, cm, base=0, flag=False):
        if flag:
            call("G", lambda e: e.iota(mk(out), pat, base, cm, allow_small_or_imprecise_dtypes=True), [out], [])
        else:
            call("G", lambda e: e.iota(mk(out), pat, base, cm), [out], [])

    def dma(q, bat, out, in_, rd, wr):
        assert bat not in closed
        rd = [(loc(b)[0], loc(b)[1] + lo, loc(b)[1] + hi, row) for b, lo, hi, row in rd]
        wr = [(loc(b)[0], loc(b)[1] + lo, loc(b)[1] + hi, row) for b, lo, hi, row in wr]
        deps(q, rd, wr)
        eng[q].dma_start(out, in_).then_inc(T.sem[bat], 16)
        dcount[bat] = dcount.get(bat, 0) + 16
        note(q, rd, wr, (bat, dcount[bat], dict(seen[q])))

    def rows(q, bat, dst, lo, hi, row, tile, c0, c1):
        b, o = loc(tile)
        dma(q, bat, T[dst][row::16, lo:hi], T[b][:, o + c0:o + c1], [(tile, c0, c1, None)], [(dst, lo, hi, row)])

    def load(q, bat, b, lo, hi, src):
        bb, o = loc(b)
        dma(q, bat, T[bb][:, o + lo:o + hi], src, [], [(b, lo, hi, None)])

    def spread(q, bat, b, lo, hi, src):
        while lo < hi:
            m = min(hi, lo + 1024)
            dma(q, bat, T[b][:, lo:m], T[src][:, 0:m - lo], [(src, 0, m - lo, None)], [(b, lo, m, None)])
            lo = m

    psn = [0]

    def bank():
        psn[0] = (psn[0] + 1) % 6
        return "ps%d" % psn[0]

    def wrap(bk, o, n, z, src, sl, w=None, r0=0, r1=16):
        zs = [z, w or z]
        lo = min(sl(r)[0] for r in range(r0, r1))
        hi = max(sl(r)[1] for r in range(r0, r1))

        def f(e):
            for r in range(r0, r1):
                zb, zo = loc(zs[r % 2])
                a, b, st = sl(r)
                rhs = T[src][:, a:b] if st == 1 else T[src][:, a:b:st]
                i = e.matmul(T[bk][:, o:o + n], T[zb][:, zo + 15 - r:zo + 143 - r], rhs, r == 0, r == 15)
            return i
        call("P", f, [A(bk)], [A(src, lo, hi)] + [A(x) for x in sorted(set(zs))])

    def wlist(bk, o, z, src, n, lo=0):
        wrap(bk, o, n // 16, z, src, lambda r: (lo + r, lo + n, 16))

    def wnat(bk, o, z, src, w):
        wrap(bk, o, 128, z, src, lambda r: (128 * r, 128 * r + 128, 1), None, 0, 8)
        wrap(bk, o, 128, z, src, lambda r: (128 * r, 128 * r + 128, 1), None, 8, 16)
        if w == 160:
            wrap(bk, o + 128, 32, z, src, lambda r: (V + 32 * r, V + 32 * r + 32, 1))

    def mm(bk, o, n, z, src, start=True, stop=True, s0=0):
        zb, zo = loc(z)
        sb, so = loc(src)
        call("P", lambda e: e.matmul(T[bk][:, o:o + n], T[zb][:, zo:zo + 128], T[sb][:, so + s0:so + s0 + n], start, stop), [A(bk)], [A(z, 0, 128), A(src, s0, s0 + n)])

    def scal(ab, lo, hi):
        b = bank()
        mm(b, 0, hi - lo, "IDN", ab, s0=lo)
        return A(b, 0, hi - lo)

    nb = [T.cores[(rank - 1) % 4], T.cores[(rank + 1) % 4]]
    lsum = [0]

    def send(src, s0, w, dst, d0, sem):
        tr = []
        for s in range(2):
            e = topo.engines(core, nb[s])
            h = len(e) // 2
            m = sum(1 << x for x in (e[:h], e[h:])[s])
            rid, pid, _ = topo.addr(nb[s])
            lsum[0] += h
            tr.append(RemoteDMATransfer(dst_ids=[DstId(rid=rid, pnc=pid)], dma_engine_mask=m, remote_sem=T.sem[sem],
                                        src=T[src][:, s0 + w * s:s0 + w * s + w], dst=T[dst][:, d0 + w * (1 - s):d0 + w * (1 - s) + w]))
        deps("G", [(src, s0, s0 + 2 * w, None)], [])
        g.remote_dma_fused(tr, local_sem=T.sem.sX)
        note("X", [], [(dst, d0, d0 + 2 * w, None)], (sem, 2 * h, dict(seen["G"])))

    load("Y", "d0", "PI", 256, 384, T.bs[:])
    load("S", "d1", "SNI", 0, 16, T.snd[:, 0:256])
    load("S", "d1", "SNI", 16, 32, T.snd[:, 256:512])
    load("Y", "d2", "PI", 128, 256, T.rt[:])
    load("Y", "d2", "PI", 0, 128, T.lt[:])
    load("S", "d3", "E", 0, V, T["err"][:])
    load("S", "d6", "ED", 0, V, T["err"][:])
    iota(A("IP"), [[0, 1]], 1)
    iota(A("IM"), [[1, 128]], 128)
    iota(A("IXX"), [[1, ZW]], 0, -15, True)
    iota(A("IM2"), [[1, 32]], 32)
    iota(A("ISi"), [[0, 2], [1, 16]], 16)
    iota(A("IL"), [[16, 160]], 1, 0, True)
    iota(A("ILs"), [[256, 2], [16, 16]], 1, P, True)
    iota(A("IK"), [[1, 128]], 0, 0, True)
    fill(A("TAB0", 0, V), -1.0)
    ts(A("MEN"), A("IM"), 2047, O.bitwise_and)
    copy(A("MHI"), A("MEN"))
    tt(A("MLO"), A("MEN"), A("MHI"), O.subtract)
    rows("Y", "d4", "TAB0", 0, V, 6, "MHI", 0, 128)
    rows("Y", "d4", "TAB0", 0, V, 7, "MLO", 0, 128)
    fill(A("SNDT0"), -1.0)
    copy(A("HI", 256, 384), A("PI", 256, 384))
    tt(A("LO", 256, 384), A("PI", 256, 384), A("HI", 256, 384), O.subtract)
    rows("Y", "d4", "TAB0", 0, V, 0, "HI", 256, 384)
    rows("Y", "d4", "TAB0", 0, V, 1, "LO", 256, 384)
    copy(A("SH"), A("SNI"))
    tt(A("SL_"), A("SNI"), A("SH"), O.subtract)
    for s in range(2):
        rows("S", "d5", "SNDT0", 16 + 288 * s, 272 + 288 * s, 0, "SH", 16 * s, 16 * s + 16)
        rows("S", "d5", "SNDT0", 16 + 288 * s, 272 + 288 * s, 1, "SL_", 16 * s, 16 * s + 16)
    copy(A("HI", 0, 256), A("PI", 0, 256))
    tt(A("LO", 0, 256), A("PI", 0, 256), A("HI", 0, 256), O.subtract)
    for a, i in ((1, 2), (0, 4)):
        rows("Y", "d4", "TAB0", 0, V, i, "HI", 128 * a, 128 * a + 128)
        rows("Y", "d4", "TAB0", 0, V, i + 1, "LO", 128 * a, 128 * a + 128)
    copy(A("pc"), A("IP"))
    ts(A("IG"), A("IP"), 112, O.bitwise_and)
    copy(A("gc"), A("IG"))
    ts(A("II"), A("IP"), 15, O.bitwise_and)
    ts(A("IJ"), A("II"), 1, O.arith_shift_right)
    copy(A("jj"), A("IJ"))
    ts(A("ZF"), A("IXX"), A("gc"), O.is_equal)

    def pick(j):
        ts(A("jc", j, j + 1), A("jj"), float(j), O.is_equal)
        ts(A(("ZB", "ZR", "ZL", "ZM")[j]), A("ZF"), A("jc", j, j + 1), O.mult)
    pick(0)
    pick(2)
    pick(1)
    load("Y", "d8", "DR", 0, 2048, T["det"][:])
    load("Y", "d9", "THI", 0, 1, T["th"][:])
    load("Y", "d9", "WTI", 0, 1, T["wt"][:])

    def consts_a():
        fill(A("TAB0", V, G), -1.0)
        ts(A("MEN2"), A("IM2"), 511, O.bitwise_and)
        for t in range(2):
            ts(A("OWN", 32 * t, 32 * t + 32), A("MEN2"), float(V + 512 * t), O.add)
        copy(A("OHI"), A("OWN"))
        tt(A("OLO"), A("OWN"), A("OHI"), O.subtract)
        rows("Y", "d7", "TAB0", V, V + 512, 2, "OHI", 0, 32)
        rows("Y", "d7", "TAB0", V, V + 512, 3, "OLO", 0, 32)

    def consts_a2():
        ts(A("MEL"), A("IL"), A("gc"), O.subtract)
        pick(3)
        fill(A("CZ"), 0.0)
        for b in ("E", "W1", "W2", "W3"):
            spread("Y", "d12", b, V, P, "CZ")
            spread("Y", "d12", b, G, WW, "CZ")
        spread("Y", "d12", "W4", V, 2576, "CZ")
        ts(A("IDN"), A("IK"), A("pc"), O.is_equal)
        ts(A("MELm"), A("MEL"), -2560.0, O.add)

    def consts_n():
        ts(A("N4K"), A("IK"), A("pc"), O.is_equal, -4096.0, O.mult)
        ts(A("mD"), A("IK"), A("gc"), O.subtract)
        ts(A("mA"), A("mD"), 0.0, O.is_ge)
        ts(A("mB"), A("mD"), 16.0, O.is_ge)
        ts(A("mE"), A("IK"), A("pc"), O.is_gt)
        tt(A("BLK"), A("mA"), A("mB"), O.subtract)
        tt(A("NLE"), A("mE"), A("mA"), O.subtract)
        ts(A("D256"), A("MEL"), 256.0, O.add)
        fill(A("ones"), 1.0)

    def consts_b():
        copy(A("PF0"), A("PI"))
        copy(A("thc"), A("THI"))
        copy(A("wtc"), A("WTI"))
        ts(A("ILs"), A("ILs"), A("gc"), O.subtract)
        copy(A("MEW", 0, 128), A("MEN"))
        copy(A("MEW", 128, 160), A("OWN", 0, 32))
        copy(A("ZA"), A("ZF"))

    def consts_c():
        ts(A("ZH"), A("ZF"), A("wtc"), O.mult)
        for t in range(2):
            ts(A("OWL", 32 * t, 32 * t + 32), A("MEL", 0, 32), float(V + 512 * t), O.add)
        ts(A("ISi"), A("ISi"), 255, O.bitwise_and)
        for s in range(2):
            ts(A("IS", 16 * s, 16 * s + 16), A("ISi", 16 * s, 16 * s + 16), float(P + 256 * s), O.add)
        for t in range(2):
            copy(A("PE", 16 * t, 16 * t + 16), A("OWN", 32 * t, 32 * t + 32, 2))
            copy(A("PE", 32 + 16 * t, 48 + 16 * t), A("OWN", 32 * t + 1, 32 * t + 32, 2))
        copy(A("PEH"), A("PE"))
        tt(A("PEL"), A("PE"), A("PEH"), O.subtract)
        fill(A("DT", 2048, 2064), -128.0)

    def consts_d(t):
        spread("Y", "d%d" % (13 + t), "NEW%d" % t, 0, G, "CZ")
        spread("Y", "d%d" % (13 + t), "MC%d" % t, 0, 512, "CZ")
        spread("Y", "d%d" % (13 + t), "CMP%d" % t, 0, 256, "CZ")
        if t == 0:
            spread("Y", "d15", "OUTR", V, P, "CZ")
            spread("Y", "d15", "NR", V, P, "CZ")
        else:
            spread("Y", "d16", "TAB1", 0, G, "CZ")
            spread("Y", "d16", "SNDT1", 0, 576, "SNDT0")
        d = "d%d" % (10 + t)
        rows("Y", d, "MC%d" % t, 0, 512, 0, "OHI", 32 * t, 32 * t + 32)
        rows("Y", d, "MC%d" % t, 0, 512, 1, "OLO", 32 * t, 32 * t + 32)
        for i, o in ((6, 0), (0, 32)):
            rows("Y", d, "CMP%d" % t, 0, 256, i, "PEH", o + 16 * t, o + 16 * t + 16)
            rows("Y", d, "CMP%d" % t, 0, 256, i + 1, "PEL", o + 16 * t, o + 16 * t + 16)
        if t == 1:
            rows("Y", d, "TAB1", 0, V, 6, "MHI", 0, 128)
            rows("Y", d, "TAB1", 0, V, 7, "MLO", 0, 128)
            rows("Y", d, "TAB1", V, V + 512, 6, "OHI", 0, 32)
            rows("Y", d, "TAB1", V, V + 512, 7, "OLO", 0, 32)
            for i in (0, 2):
                rows("Y", d, "TAB1", V + 512, P, i, "OHI", 32, 64)
                rows("Y", d, "TAB1", V + 512, P, i + 1, "OLO", 32, 64)

    late = []

    for t in range(2):
        n = V + 512 * t
        nc = n // 16
        h = n // 2
        w = 128 + 32 * t
        hh = (1024, 1536)[t]
        TAB, SNDT, NEW, MC, CMP, PF = ["%s%d" % (x, t) for x in ("TAB", "SNDT", "NEW", "MC", "CMP", "PF")]
        BB = ["BB%d%d" % (t, k) for k in range(4)]
        WB = ["E", "W1", "W2", "W3", "W4"]
        if t == 0:
            b = bank()
            wrap(b, 0, 34, "ZB", SNDT, lambda r: (16 + r, 16 + r + 544, 16))
            for s in range(2):
                copy(A("SNL", 16 * s, 16 * s + 16), A(b, 18 * s, 18 * s + 16))
            for s in range(2):
                copy(A("SNLf", 16 * s, 16 * s + 16), A(b, 18 * s, 18 * s + 16))
        else:
            late[0]()
        copy(A("OBS"), IN(TAB, 0, n, "SNL", 0, 32))
        b = bank()
        wlist(b, 0, "ZB", "OBS", 512)
        if t == 0:
            scopy(A(BB[0]), IN("E", 0, n, "SNL", 0, 32))
            consts_a()
        else:
            late[4]()
        for s in range(2):
            ts(A("gt", 16 * s, 16 * s + 16), A(b, 16 * s, 16 * s + 16), float(-(P + 256 * s) + 16), O.add, 15.0, O.max)
        for s in range(2):
            ts(A("GO%d" % t, 16 * s, 16 * s + 16), A("gt", 16 * s, 16 * s + 16), 272.0, O.min, float(288 * (1 - s)), O.add)
        send("GO%d" % t, 0, 16, "GI%d" % t, 0, "gi%d" % t)
        bl = bank()
        wlist(bl, 0, "ZL", TAB, n)
        br = bank()
        wlist(br, 0, "ZR", TAB, n)
        bb = bank()
        wlist(bb, 0, "ZB", TAB, n)
        if t == 1:
            late[1]()
            late[2]()
            late[3]()
            scopy(A(BB[0]), IN("E", 0, n, "SNL", 0, 32))
        send(BB[0], 0, 256, "E", P, "ga%d0" % t)
        if t == 0:
            consts_a2()
        copy(A("LL", 0, nc), A(bl, 0, nc))
        ts(A("LM", 0, nc), A(bl, 0, nc), float(-G), O.add)
        if t == 0:
            consts_n()
        copy(A("RL", 0, nc), A(br, 0, nc))
        ts(A("RM", 0, nc), A(br, 0, nc), float(-G), O.add)
        if t == 0:
            consts_b()
            slin(A("DX"), A("DR"), 0.5, 127.8)
        copy(A(TAB, P, G), IN(SNDT, 0, 576, "GI%d" % t, 0, 32))
        b1 = bank()
        b2 = bank()
        for j in range(2):
            copy(A("OUTL", h * j, h * j + h), IN(TAB, 0, G, "LL", nc // 2 * j, nc // 2 * j + nc // 2))
            scopy(A("OUTR", h * j, h * j + h), IN(TAB, 0, G, "RL", nc // 2 * j, nc // 2 * j + nc // 2))
            wlist(b1, nc // 2 * j, "ZB", "OUTL", h, h * j)
            wlist(b2, nc // 2 * j, "ZB", "OUTR", h, h * j)
        ts(A("BL", 0, nc), A(bb, 0, nc), float(P - 1), O.min)
        ts(A("BLm", 0, nc), A(bb, 0, nc), -2560.0, O.add)
        copy(A("OSL"), IN("OUTL", 0, n, "SNL", 0, 32))
        scopy(A("OSR"), IN("OUTR", 0, n, "SNL", 0, 32))
        bs = bank()
        wlist(bs, 0, "ZL", "OBS", 512)
        wlist(bs, 32, "ZR", "OBS", 512)
        b3 = bank()
        wlist(b3, 0, "ZB", "OSL", 512)
        wlist(b3, 32, "ZB", "OSR", 512)
        scopy(A("OUTB", 0, n), IN(TAB, 0, G, "BL", 0, nc))
        if t == 0:
            slin(A("DT", 0, 2048), A("DX"), 1.0, -256.0)

        def valid(bk, o, me, lm, gl, k):
            x, y = ("ea", "pa") if gl in ("GL", "SL") else ("eb", "pb")
            tt(A(x, 0, k), A(bk, o, o + k), A(me, 0, k), O.is_equal)
            tt(A(y, 0, k), A(x, 0, k), A(lm, 0, k), O.mult)
            ts(A(gl, 0, k), A(y, 0, k), float(G), O.add)

        if t == 0:
            consts_c()
        valid(b2, 0, "MEL", "RM", "GR", nc)
        valid(b1, 0, "MEL", "LM", "GL", nc)
        for k in range(4):
            wi, wo = WB[k], WB[k + 1]
            nchunk = n // 512
            na = nchunk - NCH[t][k]
            for x, c in [("R", c) for c in range(na)] + [(x, c) for c in range(na, nchunk) for x in "LR"]:
                scopy(A("AB" if x == "R" else "AC", 512 * c, 512 * c + 512), IN(wi, 0, WW, "G" + x, 32 * c, 32 * c + 32))

            def xs(c0, c1):
                if c0 < c1:
                    tt(A("X", 512 * c0, 512 * c1), IN(wi, 0, WW, "GL", 32 * c0, 32 * c1), A("ED", 512 * c0, 512 * c1), O.max)
            c0 = 0
            if k == 0:
                c0 = 1
                xs(0, 1)
                ts(A("SLM"), A(bs, 0, 32), float(-G), O.add)
                ts(A("SRM"), A(bs, 32, 64), float(-G), O.add)
                if t == 0:
                    tt(A("RSq"), A(bs, 32, 64), A("ILs"), O.is_equal)
                valid(b3, 0, "SNLf", "SLM", "SL", 32)
                valid(b3, 32, "SNLf", "SRM", "SR", 32)
            if k < 3:
                tt(A("M", 0, 512), IN(wi, 0, WW, "SL", 0, 32), A(BB[k]), O.max)
                tt(A(BB[k + 1]), IN(wi, 0, WW, "SR", 0, 32), A("M", 0, 512), O.max)
                send(BB[k + 1], 0, 256, WB[k + 1], P, "ga%d%d" % (t, k + 1))
            xs(c0, na)
            for c in range(nchunk):
                lo, hi = 512 * c, 512 * c + 512
                if c >= na:
                    tt(A("X", lo, hi), A("ED", lo, hi), scal("AC", lo, hi), O.max)
                tt(A(wo, lo, hi), A("X", lo, hi), scal("AB", lo, hi), O.max)
                if k == 3 and hi <= hh:
                    scopy(A("WD", lo, hi), A(wo, lo, hi))
            if k == 1:
                if t == 0:
                    consts_d(0)
                wlist("ps6", 0, "ZB", "OUTB", n)
                if t == 0:
                    for s in range(2):
                        wrap("ps6", 160 + 16 * s, 16, "ZR", "OBS", lambda r: (256 * s + 16 * r, 256 * s + 16 * r + 16, 1))
            if k == 2:
                if t == 0:
                    tt(A("RSn"), A("ps6", 160, 192), A("IS"), O.is_equal)
                tt(A("pr", 0, nc), A("ps6", 0, nc), A("MEL", 0, nc), O.is_equal)
                tt(A("pt", 0, nc), A("BLm", 0, nc), A("pr", 0, nc), O.mult)
                ts(A("PB", 0, nc), A("pt", 0, nc), 2560.0, O.add)
                tt(A("pa", 0, nc), A("MELm", 0, nc), A("BLm", 0, nc), O.is_lt)
                tt(A("pa", 0, nc), A("pa", 0, nc), A("pr", 0, nc), O.mult)
                ts(A("TH9", 0, nc), A("pa", 0, nc), -1000.0, O.mult, float(Q + 1000), O.add)
            if k == 2 and t == 0:
                consts_d(1)
            if k < 3:
                wnat("ps7", w * k, "ZR", ("OUTL", "OUTR", "OUTB")[k], w)
            if k == 3:
                for a in range(3):
                    tt(A("F3", a * w, a * w + w), A("ps7", a * w, a * w + w), A("MEW", 0, w), O.is_equal)
        scopy(A("AC", hh, n), IN("W4", 0, 2576, "PB", hh // 16, nc))
        bm = bank()
        tt(A("M", 0, hh), IN("W4", 0, 2576, "PB", 0, hh // 16), A("WD", 0, hh), O.max)
        ts(A("FL", 0, hh), A("M", 0, hh), A("thc"), O.is_ge)
        parts = [(lo, hi, scal("AC", lo, hi)) for lo, hi in ((hh, hh + 512), (hh + 512, n))]
        wlist(bm, 0, "ZA", "FL", hh)
        for lo, hi, ps in parts:
            tt(A("M", lo, hi), A("W4", lo, hi), ps, O.max)
            ts(A("FL", lo, hi), A("M", lo, hi), A("thc"), O.is_ge)
        wlist(bm, hh // 16, "ZA", "FL", n - hh, hh)
        tt(A("go", 0, nc), A(bm, 0, nc), A("TH9", 0, nc), O.is_ge)
        b = bank()
        b2 = bank()
        mm(b, 0, nc, "BLK", "go")
        mm(b2, 0, nc, "NLE", "go", True, False)
        mm(b2, 0, nc, "N4K", "go", False, True)
        call("V", lambda e: e.tensor_tensor_scan(mk(A("sc", 0, nc)), mk(A("ones", 0, nc)), mk(A(b, 0, nc)), 4096.0, O.mult, O.add), [A("sc", 0, nc)], [A("ones", 0, nc), A(b, 0, nc)])
        tt(A("kk", 0, nc), A(b2, 0, nc), A("sc", 0, nc), O.add)
        ts(A("c8", 0, nc), A("kk", 0, nc), 256.0, O.is_ge, 8192.0, O.mult)
        tt(A("kk", 0, nc), A("kk", 0, nc), A("c8", 0, nc), O.add)
        tt(A("c8", 0, nc), A("kk", 0, nc), A("D256", 0, nc), O.min)
        copy(A("TG", 0, nc), A("c8", 0, nc))
        copy(IN(CMP, 0, 256 + n, "TG", 0, nc), A(TAB, 0, n))
        b = bank()
        wrap(b, 0, 32, "ZM", CMP, lambda r: (r >> 1, 256, 8), "ZB")
        copy(A("TD"), A(b, 0, 32))
        copy(IN(NEW, 0, G, "TD", 0, 32), A(MC))
        copy(A("TF"), A(b, 0, 32))
        bh = "ps7"

        def errs():
            scopy(A("ET"), IN("E", 0, P, "TD", 0, 32))
            wlist(bh, 0, "ZH", "ET", 512)

        if t == 1:
            errs()
        scopy(A("OT"), IN(TAB, 0, G, "TD", 0, 32))
        scopy(A("ORT"), IN("OUTR", 0, P, "TD", 0, 32))
        (copy, scopy)[t](A("NR", 0, 1024), IN(NEW, 0, G, "RL", 0, 64))
        scopy(A("NR", 1024, n), IN(NEW, 0, G, "RL", 64, nc))
        for lo, hi in ((0, 1024), (1024, n)):
            copy(A("NB", lo, hi), IN(NEW, 0, G, "BL", lo // 16, hi // 16))
            scopy(A("NL", lo, hi), IN(NEW, 0, G, "LL", lo // 16, hi // 16))
        bn = bank()
        wrap(bn, 0, 16, "ZM", CMP, lambda r: (16 * r, 16 * r + 16, 1))
        wrap(bn, 16, 16, "ZB", CMP, lambda r: (16 * r, 16 * r + 16, 1))
        bo = bank()
        wnat(bo, 0, "ZB", NEW, w)
        bR, bB, bL = bank(), bank(), bank()
        wnat(bR, 0, "ZB", "NR", w)
        wnat(bB, 0, "ZB", "NB", w)
        wnat(bL, 0, "ZB", "NL", w)
        scopy(A("ONT"), IN("NR", 0, P, "TD", 0, 32))
        if t == 0:
            scopy(A("ONS"), IN(NEW, 0, G, "SNL", 0, 32))
            errs()
        for x in range(2):
            copy(A("TN", x, 32, 2), A(bn, 16 * x, 16 * x + 16))
            copy(A("ON", 1 - x, 32, 2), A(bn, 16 * x, 16 * x + 16))
        ts(A("nz", 0, w), A(bo, 0, w), 0.0, O.is_equal)
        ts(A("zz", 0, w), A(bo, 0, w), 0.0, O.is_gt)
        copy(A("nq", 0, w), A(bo, 0, w))

        def err0(t=t, n=n):
            tt(A("hx", 0, 32), A(bh, 0, 32), A("TF"), O.add)
            tt(A("hx", 32, 64), A(bh, 0, 32), A("OWL", 32 * t, 32 * t + 32), O.add)
            ts(A("hy"), A("hx"), 2047, O.bitwise_and)
            ts(A("em"), A("TF"), float(n), O.is_ge, 2048.0, O.mult)
            for x in range(2):
                tt(A("hz", 32 * x, 32 * x + 32), A("hy", 32 * x, 32 * x + 32), A("em"), O.max)
            copy(A("HX"), A("hz"))
            ts(A("E2"), A("ET"), 0.5, O.mult, 127.8, O.add)
            tt(A("CL"), IN("DT", 0, 2064, "HX", 0, 32), A("E2"), O.add)

        def err1(n=n):
            tt(A("E", n, n + 512), IN("DT", 0, 2064, "HX", 32, 64), A("E2"), O.add)

        def err2():
            copy(IN("E", 0, P, "TD", 0, 32), A("CL"))

        def err3():
            dma("Y", "d25", T["ED"][:], T["E"][:, 0:2560], [("E", 0, 2560, None)], [("ED", 0, 2560, None)])

        late = [err0, err2, err1, err3]
        if t == 1:
            err0()
            err2()
            err1()
            dma("Y", "d30", T["ye"][:], T["E"][:, 0:P], [("E", 0, P, None)], [])
        PN = "PF%d" % (t + 1)
        wn = w + 32
        q = [A("q3", a * w, a * w + w) for a in range(3)]
        pn = [A(PN, a * wn, a * wn + w) for a in range(3)]
        nw = [A(PN, a * wn + w, a * wn + wn) for a in range(3)]
        own = A("OWN", 32 * t, 32 * t + 32)
        tt(q[1], A(bR, 0, w), A("F3", w, 2 * w), O.mult)
        tt(q[2], A(bB, 0, w), A("F3", 2 * w, 3 * w), O.mult)
        tt(A("pz", 0, w), A(bB, 0, w), A("zz", 0, w), O.mult)
        tt(q[0], A(bL, 0, w), A("F3", 0, w), O.mult)
        tt(A("q3", 0, 3 * w), A("q3", 0, 3 * w), A(PF), O.max)
        tt(A("zz", 0, w), A("zz", 0, w), q[0], O.mult)
        for a in range(3):
            tt(pn[a], q[a], A("nz", 0, w), O.mult)
        for a, x in ((0, "nq"), (1, "pz"), (2, "zz")):
            tt(pn[a], pn[a], A(x, 0, w), O.add)
        bq = bank()
        wrap(bq, 0, 32, "ZR", "OT", lambda r: (32 * r, 32 * r + 32, 1))
        wrap(bq, 32, 32, "ZR", "ORT", lambda r: (32 * r, 32 * r + 32, 1))
        wrap(bq, 64, 32, "ZB", "ONT", lambda r: (32 * r, 32 * r + 32, 1))
        copy(nw[1], A("TN"))
        ts(A("e2"), A("TN"), float(n), O.is_ge)
        tt(A("e3"), own, A("ON"), O.subtract)
        tt(A("e3"), A("e3"), A("e2"), O.mult)
        tt(nw[0], A("ON"), A("e3"), O.add)
        tt(A("e1"), A(bq, 32, 64), A("TN"), O.is_equal)
        tt(A("e1"), A(bq, 64, 96), A("e1"), O.mult)
        tt(nw[2], A(bq, 0, 32), A("e1"), O.max)
        if t == 1:
            for a, y in enumerate(("yl", "yr", "yb")):
                for lo, hi, c0, c1 in ((0, V, 0, 128), (V, V + 512, 128, 160), (V + 512, P, 160, 192)):
                    dma("YSY"[a], "d31", T[y][:, lo:hi], T[PN][:, a * wn + c0:a * wn + c1], [(PN, a * wn, a * wn + wn, None)], [])
            break
        copy(A("HI1"), A(PN))
        tt(A("LO1"), A(PN), A("HI1"), O.subtract)
        for a, i in ((2, 0), (1, 2), (0, 4)):
            for hl, x in enumerate(("HI1", "LO1")):
                rows("YS"[hl], "d20", "TAB1", 0, V, i + hl, x, a * wn, a * wn + w)
                rows("YS"[hl], "d20", "TAB1", V, V + 512, i + hl, x, a * wn + w, a * wn + wn)
        bs = bank()
        wlist(bs, 0, "ZB", "ONS", 512)
        tt(A("sq"), A(bs, 0, 32), A("RSq"), O.mult)
        tt(A("SNLf"), A("SNLf"), A("sq"), O.max)
        copy(A("SNL"), A("SNLf"))
        for s in range(2):
            wrap("ps6", 16 * s, 16, "ZB", "ONS", lambda r: (256 * s + 16 * r, 256 * s + 16 * r + 16, 1))

        def snd_rows():
            tt(A("sq"), A("ps6", 0, 32), A("RSn"), O.mult)
            tt(A("SN1"), A("sq"), A("SNI"), O.max)
            copy(A("SH1"), A("SN1"))
            tt(A("SL1"), A("SN1"), A("SH1"), O.subtract)
            for s in range(2):
                rows("Y", "d24", "SNDT1", 16 + 288 * s, 272 + 288 * s, 0, "SH1", 16 * s, 16 * s + 16)
                rows("Y", "d24", "SNDT1", 16 + 288 * s, 272 + 288 * s, 1, "SL1", 16 * s, 16 * s + 16)
        late.append(snd_rows)
    for d in sorted(dcount):
        wait("Y", (d, dcount[d], {}))
    for q in ("V", "S", "P", "G"):
        wait("Y", ("s" + q, count[q], {}))
    g.wait_ge(T.sem.sX, lsum[0])
